import numpy as np
import ml_dtypes


def mxq(x, axis, fmt="e4m3"):
    dtype, down = {"e4m3": (ml_dtypes.float8_e4m3fn, 7), "e5m2": (ml_dtypes.float8_e5m2, 14)}[fmt]
    v = np.moveaxis(np.asarray(x, np.float32).astype(ml_dtypes.bfloat16).astype(np.float64), axis, -1)
    blocks = v.reshape(v.shape[:-1] + (-1, 32))
    amax = np.abs(blocks).max(-1, keepdims=True)
    byte = np.maximum(np.where(amax > 0, np.frexp(amax)[1] - 1 + 127, 0) - down, 1)
    scale = np.exp2(byte - 127.0)
    codes = (blocks / scale).astype(np.float32).astype(dtype).astype(np.float64)
    return np.moveaxis((codes * scale).reshape(v.shape), -1, axis)


WIDE = False


def mx_kscale(k):
    if not WIDE:
        return np.ones(k)
    levels = np.array([10, -10, 5, -5, 0])
    if k % 512:
        return np.exp2(np.random.permutation(np.resize(levels, k // 32))).repeat(32)
    a = np.empty((k // 512, 16))
    for p in range(k // 512):
        a[p, :8] = np.random.permutation(np.resize(levels, 8))
        for g in range(8):
            far = levels[np.abs(levels - a[p, g]) >= 10]
            a[p, g + 8] = far[np.random.randint(len(far))]
    return np.exp2(a.ravel()).repeat(32)


BF16 = ml_dtypes.bfloat16


def bf(x):
    return np.asarray(x, np.float32).astype(BF16)


def f64(x):
    return np.asarray(x).astype(np.float64)


E2M1 = np.array([0.0, 0.5, 1.0, 1.5, 2.0, 3.0, 4.0, 6.0, -0.0, -0.5, -1.0, -1.5, -2.0, -3.0, -4.0, -6.0])


def pack_weight(w, fmt):
    k, n = w.shape
    w = f64(bf(w)).reshape(k // 32, 32, n)
    amax = np.abs(w).max(1)
    if fmt == "e4m3":
        byte = np.frexp(amax)[1] - 1 + 127 - 7
    else:
        mant, ex = np.frexp(amax / 6.0)
        byte = np.where(mant > 0.5, ex, ex - 1) + 127
    byte = np.clip(np.where(amax > 0, byte, 1), 1, 254)
    scaled = (w * np.exp2(127.0 - byte)[:, None, :]).reshape(k, n).astype(np.float32)
    by_word = np.ascontiguousarray(scaled.reshape(k // 512, 128, 4, n).transpose(0, 1, 3, 2))
    if fmt == "e4m3":
        words = by_word.astype(ml_dtypes.float8_e4m3fn).view(np.uint8)
    else:
        c = by_word.astype(ml_dtypes.float4_e2m1fn).view(np.uint8) & 0xF
        words = c[..., 0::2] | (c[..., 1::2] << 4)
    return np.ascontiguousarray(words), np.ascontiguousarray(byte.astype(np.uint8).reshape(k // 512, 16, n))


def unpack_weight(words, scales, fmt):
    g, p, n, _ = words.shape
    if fmt == "e4m3":
        vals = np.ascontiguousarray(words).view(ml_dtypes.float8_e4m3fn).astype(np.float64)
    else:
        nib = np.empty((g, p, n, 4), np.uint8)
        nib[..., 0::2] = words & 0xF
        nib[..., 1::2] = words >> 4
        vals = E2M1[nib]
    vals = vals * np.repeat(np.exp2(scales.astype(np.float64) - 127.0), 8, axis=1)[..., None]
    return vals.transpose(0, 1, 3, 2).reshape(g * 512, n)
def pack4(w):
    words, scales = pack_weight(w, "e2m1")
    return words.reshape(words.shape[0], 128, -1), scales


def unpack4(words, scales):
    return unpack_weight(words.reshape(words.shape[0], 128, -1, 2), scales, "e2m1")


M, K, N, F = 1024, 1024, 2048, 1024


def setup_inputs():
    s, t = mx_kscale(K), mx_kscale(N)
    past = np.random.standard_normal((K, M)) * s[:, None]
    pinv = np.random.standard_normal((K, N)) / np.sqrt(K) / s[:, None] * t
    fut = np.random.standard_normal((N, F)) / np.sqrt(N) / t[:, None]
    past_words, past_scales = pack4(past)
    pinv_words, pinv_scales = pack4(pinv)
    fut_words, fut_scales = pack_weight(fut, "e4m3")
    return {"past_words": past_words, "past_scales": past_scales,
            "pinv_words": pinv_words, "pinv_scales": pinv_scales,
            "box": bf(np.random.uniform(0.6, 1.8, N) * t),
            "fut_words": fut_words, "fut_scales": fut_scales,
            "offset": bf(0.5 * np.random.standard_normal(F))}


def reference(past_words, past_scales, pinv_words, pinv_scales, box, fut_words, fut_scales, offset):
    x = unpack4(past_words, past_scales)
    v = unpack4(pinv_words, pinv_scales)
    h = unpack_weight(fut_words, fut_scales, "e4m3")
    c = f64(box)
    a = x.T @ v
    a = np.maximum(np.minimum(a, c), -c)
    y = mxq(a, 1, "e4m3") @ h
    return y + f64(offset)

@@ -1,0 +1,269 @@
+from contextlib import ExitStack
+
+import concourse.mybir as mybir
+
+M, K, N, F = 1024, 1024, 2048, 1024
+FLOPS = 2 * M * K * N + 2 * M * N * F
+BYTES = 8034304
+
+F32 = mybir.dt.float32
+BF16 = mybir.dt.bfloat16
+U32 = mybir.dt.uint32
+I32 = mybir.dt.int32
+U8 = mybir.dt.uint8
+FP8X4 = mybir.dt.float8_e4m3fn_x4
+FP4X4 = mybir.dt.float4_e2m1fn_x4
+ALU = mybir.AluOpType
+
+P = 128
+
+
+def tile_behavioural_box_predictor_s4_kernel(
+    tc, past_words, past_scales, pinv_words, pinv_scales, box, fut_words, fut_scales, offset, out
+):
+    nc = tc.nc
+    with ExitStack() as ctx:
+        keep = ctx.enter_context(tc.tile_pool(name="keep", bufs=1))
+        work = ctx.enter_context(tc.tile_pool(name="work", bufs=3))
+        psum = ctx.enter_context(tc.psum_pool(name="psum", bufs=8))
+
+        def kept(shape, dtype, name):
+            return keep.tile(shape, dtype, name=name, tag=name, align_bytes=256)
+
+        vw0 = kept([P, 2, 1024], U8, "vw0")
+        vw1 = kept([P, 2, 1024], U8, "vw1")
+        vw23 = kept([P, 2, 2048], U8, "vw23")
+        vs_ab = [kept([P, 2, 1024], U8, "vs%d" % i) for i in range(2)]
+        xw = [kept([P, 2, 1024], U8, "xw%d" % i) for i in range(2)]
+        xs = kept([P, 2, 1024], U8, "xs")
+        vp = [kept([P, 4, 2, 256], U8, "vp%d" % c) for c in range(4)]
+        vsp = [kept([P, 4, 2, 128], U8, "vsp%d" % c) for c in range(4)]
+        hw = [kept([P, 4096], U8, "hw%d" % g) for g in range(4)]
+        hs = kept([P, 1024], U8, "hs")
+        box_bf = kept([P, 4, 4], BF16, "box_bf")
+        hi = kept([P, 16], F32, "hi")
+        lo = kept([P, 16], F32, "lo")
+        off = kept([P, 1024], BF16, "off")
+        bc = [[kept([P, 512], U32, "bc%d_%d" % (h, c)) for c in range(4)] for h in range(2)]
+        bs = [[kept([P, 512], U8, "bs%d_%d" % (h, c)) for c in range(4)] for h in range(2)]
+
+        def raw(c):
+            if c == 0:
+                return vw0[:]
+            if c == 1:
+                return vw1[:]
+            return vw23[:, :, 1024 * (c - 2) : 1024 * (c - 1)]
+
+        pw = pinv_words.rearrange("g p b -> p g b")
+        xwr = past_words.rearrange("g p b -> p g b")
+
+        def load(eng, dst, src):
+            eng.dma_start(out=dst.bitcast(I32), in_=src.bitcast(I32))
+
+        def scale_rows(eng, dst, src, q):
+            load(eng, dst[32 * q : 32 * q + 4], src[:, 4 * q : 4 * q + 4, :].rearrange("g r n -> r g n"))
+
+        with tc.manual_schedule():
+            load(nc.sync, vw0[:], pw[:, :, 0:1024])
+            load(nc.gpsimd, xw[0][:], xwr[:, :, 0:1024])
+            nc.vector.memset(vs_ab[0][:].bitcast(I32), 0)
+            nc.vector.memset(xs[:].bitcast(I32), 0)
+            nc.vector.memset(vs_ab[1][:].bitcast(I32), 0)
+            for q in range(4):
+                scale_rows(nc.sync, vs_ab[0], pinv_scales[:, :, 0:1024], q)
+            for q in range(3):
+                scale_rows(nc.sync, xs, past_scales, q)
+            scale_rows(nc.gpsimd, xs, past_scales, 3)
+            load(nc.gpsimd, vw1[:], pw[:, :, 1024:2048])
+            load(nc.sync, vw23[:], pw[:, :, 2048:4096])
+            for q in range(4):
+                scale_rows(nc.sync, vs_ab[1], pinv_scales[:, :, 1024:2048], q)
+            nc.sync.dma_start(out=box_bf[:], in_=box.rearrange("(c p t) -> p c t", p=P, t=4))
+            load(nc.sync, xw[1][:], xwr[:, :, 1024:2048])
+            nc.gpsimd.memset(hs[:].bitcast(I32), 0)
+            for g in range(4):
+                load(nc.sync, hw[g][:], fut_words[g].rearrange("p n t -> p (n t)"))
+            for q in range(4):
+                load(nc.sync, hs[32 * q : 32 * q + 16, :], fut_scales[:, 4 * q : 4 * q + 4, :])
+            nc.sync.dma_start(out=off[:], in_=offset.partition_broadcast(P))
+
+            def permute(c):
+                scales = vs_ab[c // 2][:, :, 512 * (c % 2) : 512 * (c % 2 + 1)]
+                if c == 0:
+                    for t in range(4):
+                        nc.vector.tensor_copy(
+                            out=vp[c][:, t].rearrange("p g (m b) -> p g m b", b=2),
+                            in_=raw(c).rearrange("p g (m t b) -> p t g m b", t=4, b=2)[:, t],
+                        )
+                        nc.vector.tensor_copy(
+                            out=vsp[c][:, t], in_=scales.rearrange("p g (m t) -> p t g m", t=4)[:, t]
+                        )
+                else:
+                    for g in range(2):
+                        nc.vector.tensor_copy(
+                            out=vp[c][:, :, g].rearrange("p t (m b) -> p t m b", b=2),
+                            in_=raw(c)[:, g].rearrange("p (m t b) -> p t m b", t=4, b=2),
+                        )
+                    nc.vector.tensor_copy(out=vsp[c][:], in_=scales.rearrange("p g (m t) -> p t g m", t=4))
+
+            s32 = {}
+            cl = {}
+            gr = {}
+
+            def stage1(h, c):
+                s32[h, c] = work.tile([P, 4, 512], F32, name="s32", tag="s32", bufs=6, align_bytes=256)
+                for t in range(4):
+                    ps = psum.tile([P, 512], F32, name="ps", tag="ps")
+                    for g in range(2):
+                        nc.tensor.matmul_mx(
+                            out=ps[:],
+                            lhsT=vp[c][:, t, g, :].bitcast(FP4X4),
+                            lhsT_scale=vsp[c][:, t, g, :],
+                            rhs=xw[h][:, g, :].bitcast(FP4X4),
+                            rhs_scale=xs[:, g, 512 * h : 512 * h + 512],
+                            start=(g == 0),
+                            stop=(g == 1),
+                        )
+                    nc.scalar.copy(out=s32[h, c][:, t, :], in_=ps[:])
+
+            def clamp(h, c, t):
+                if t == 0:
+                    cl[h, c] = work.tile([P, 4, 512], BF16, name="cl", tag="cl", bufs=5, align_bytes=256)
+                j = 4 * c + t
+                nc.vector.tensor_scalar(
+                    out=cl[h, c][:, t, :],
+                    in0=s32[h, c][:, t, :],
+                    scalar1=hi[:, j : j + 1],
+                    scalar2=lo[:, j : j + 1],
+                    op0=ALU.min,
+                    op1=ALU.max,
+                )
+
+            def weave(h, c, k, eng):
+                if k == 0:
+                    gr[h, c] = work.tile([P, 512, 4], BF16, name="gr", tag="gr", bufs=4, align_bytes=256)
+                cols = slice(256 * k, 256 * k + 256)
+                dst = gr[h, c][:, cols, :]
+                src = cl[h, c][:, :, cols].rearrange("p t m -> p m t")
+                if eng == "v":
+                    nc.vector.tensor_copy(out=dst, in_=src)
+                else:
+                    nc.scalar.copy(out=dst, in_=src)
+
+            def quantize(h, c, k):
+                cols = slice(256 * k, 256 * k + 256)
+                nc.vector.quantize_mx(
+                    out=bc[h][c][:, cols].bitcast(FP8X4),
+                    scales=bs[h][c][:, cols],
+                    in_=gr[h, c][:, cols, :].rearrange("p m t -> p (m t)"),
+                )
+
+            acc = {}
+
+            def mm2(i, f, g, first, last):
+                h, cols = i // 4, slice(128 * (i % 4), 128 * (i % 4) + 128)
+                if first:
+                    acc[i, f] = psum.tile([P, 512], F32, name="ps", tag="ps")
+                nc.tensor.matmul_mx(
+                    out=acc[i, f][:],
+                    lhsT=bc[h][g][:, cols].bitcast(FP8X4),
+                    lhsT_scale=bs[h][g][:, cols],
+                    rhs=hw[g][:, 2048 * f : 2048 * f + 2048].bitcast(FP8X4),
+                    rhs_scale=hs[4 * g : P, 512 * f : 512 * f + 512],
+                    start=first,
+                    stop=last,
+                )
+
+            ot = {}
+
+            def finish(i, f):
+                if f == 0:
+                    ot[i] = work.tile([P, 1024], F32, name="ot", tag="ot", bufs=4, align_bytes=256)
+                cols = slice(512 * f, 512 * f + 512)
+                nc.vector.tensor_tensor(out=ot[i][:, cols], in0=acc[i, f][:], in1=off[:, cols], op=ALU.add)
+                if i == 7:
+                    nc.sync.dma_start(out=out[P * i : P * i + P, cols], in_=ot[i][:, cols])
+                elif f == 1:
+                    nc.sync.dma_start(out=out[P * i : P * i + P, :], in_=ot[i][:])
+
+            def stage2_block(i0, order, group_major):
+                tiles = [(i, f) for i in (i0, i0 + 1) for f in range(2)]
+                if group_major:
+                    for n, g in enumerate(order):
+                        for i, f in tiles:
+                            mm2(i, f, g, n == 0, n == 3)
+                else:
+                    for i, f in tiles:
+                        for n, g in enumerate(order):
+                            mm2(i, f, g, n == 0, n == 3)
+
+            def pipe(new, old, eng):
+                clamp(*new, 0)
+                clamp(*new, 1)
+                weave(*old, 0, "v")
+                clamp(*new, 2)
+                weave(*old, 1, "v")
+                clamp(*new, 3)
+                quantize(*old, 0)
+                quantize(*old, 1)
+
+            permute(0)
+            stage1(0, 0)
+            permute(1)
+            stage1(0, 1)
+            permute(2)
+            nc.vector.tensor_scalar(out=hi[:], in0=box_bf[:].rearrange("p c t -> p (c t)"), scalar1=1.0, scalar2=None, op0=ALU.mult)
+            nc.vector.tensor_scalar(out=lo[:], in0=box_bf[:].rearrange("p c t -> p (c t)"), scalar1=-1.0, scalar2=None, op0=ALU.mult)
+            permute(3)
+            for t in range(4):
+                clamp(0, 0, t)
+            stage1(0, 2)
+            stage1(0, 3)
+            pipe((0, 1), (0, 0), "v")
+            stage1(1, 0)
+            pipe((0, 2), (0, 1), "v")
+            stage1(1, 1)
+            pipe((0, 3), (0, 2), "v")
+            stage1(1, 2)
+            pipe((1, 0), (0, 3), "v")
+            stage1(1, 3)
+            stage2_block(0, (0, 1, 2, 3), True)
+            weave(1, 0, 0, "s")
+            weave(1, 0, 1, "s")
+            for t in range(4):
+                clamp(1, 1, t)
+            weave(1, 1, 0, "s")
+            weave(1, 1, 1, "s")
+            for t in range(4):
+                clamp(1, 2, t)
+            weave(1, 2, 0, "s")
+            weave(1, 2, 1, "s")
+            quantize(1, 0, 0)
+            quantize(1, 0, 1)
+            for t in range(4):
+                clamp(1, 3, t)
+            finish(0, 0)
+            weave(1, 3, 0, "v")
+            finish(0, 1)
+            weave(1, 3, 1, "v")
+            quantize(1, 3, 0)
+            finish(1, 0)
+            quantize(1, 3, 1)
+            finish(1, 1)
+            quantize(1, 1, 0)
+            quantize(1, 1, 1)
+            stage2_block(2, (0, 1, 2, 3), False)
+            finish(2, 0)
+            finish(2, 1)
+            quantize(1, 2, 0)
+            quantize(1, 2, 1)
+            finish(3, 0)
+            finish(3, 1)
+            stage2_block(4, (0, 1, 3, 2), True)
+            for i in (4, 5):
+                for f in range(2):
+                    finish(i, f)
+            stage2_block(6, (0, 1, 2, 3), False)
+            for i in (6, 7):
+                for f in range(2):
+                    finish(i, f)

@@ -33,9 +33,10 @@ def tile_behavioural_box_predictor_s4_kernel(
         vw0 = kept([P, 2, 1024], U8, "vw0")
         vw1 = kept([P, 2, 1024], U8, "vw1")
         vw23 = kept([P, 2, 2048], U8, "vw23")
-        vs_ab = [kept([P, 2, 1024], U8, "vs%d" % i) for i in range(2)]
+        vs0 = kept([P, 2, 512], U8, "vs0")
+        vs123 = kept([P, 2, 1536], U8, "vs123")
         xw = [kept([P, 2, 1024], U8, "xw%d" % i) for i in range(2)]
-        xs = kept([P, 2, 1024], U8, "xs")
+        xs = [kept([P, 2, 512], U8, "xs%d" % i) for i in range(2)]
         vp = [kept([P, 4, 2, 256], U8, "vp%d" % c) for c in range(4)]
         vsp = [kept([P, 4, 2, 128], U8, "vsp%d" % c) for c in range(4)]
         hw = [kept([P, 4096], U8, "hw%d" % g) for g in range(4)]
@@ -64,23 +65,23 @@ def tile_behavioural_box_predictor_s4_kernel(
             load(eng, dst[32 * q : 32 * q + 4], src[:, 4 * q : 4 * q + 4, :].rearrange("g r n -> r g n"))
 
         with tc.manual_schedule():
-            load(nc.sync, vw0[:], pw[:, :, 0:1024])
+            load(nc.gpsimd, vw0[:], pw[:, :, 0:1024])
             load(nc.gpsimd, xw[0][:], xwr[:, :, 0:1024])
-            nc.vector.memset(vs_ab[0][:].bitcast(I32), 0)
-            nc.vector.memset(xs[:].bitcast(I32), 0)
-            nc.vector.memset(vs_ab[1][:].bitcast(I32), 0)
+            for plane in (vs0, xs[0], vs123, xs[1]):
+                nc.vector.memset(plane[:].bitcast(I32), 0)
             for q in range(4):
-                scale_rows(nc.sync, vs_ab[0], pinv_scales[:, :, 0:1024], q)
-            for q in range(3):
-                scale_rows(nc.sync, xs, past_scales, q)
-            scale_rows(nc.gpsimd, xs, past_scales, 3)
-            load(nc.gpsimd, vw1[:], pw[:, :, 1024:2048])
+                scale_rows(nc.sync, vs0, pinv_scales[:, :, 0:512], q)
+            for q in range(4):
+                scale_rows(nc.scalar, xs[0], past_scales[:, :, 0:512], q)
+            nc.gpsimd.memset(hs[:].bitcast(I32), 0)
+            load(nc.sync, vw1[:], pw[:, :, 1024:2048])
             load(nc.sync, vw23[:], pw[:, :, 2048:4096])
             for q in range(4):
-                scale_rows(nc.sync, vs_ab[1], pinv_scales[:, :, 1024:2048], q)
+                scale_rows(nc.sync, vs123, pinv_scales[:, :, 512:2048], q)
             nc.sync.dma_start(out=box_bf[:], in_=box.rearrange("(c p t) -> p c t", p=P, t=4))
             load(nc.sync, xw[1][:], xwr[:, :, 1024:2048])
-            nc.gpsimd.memset(hs[:].bitcast(I32), 0)
+            for q in range(4):
+                scale_rows(nc.sync, xs[1], past_scales[:, :, 512:1024], q)
             for g in range(4):
                 load(nc.sync, hw[g][:], fut_words[g].rearrange("p n t -> p (n t)"))
             for q in range(4):
@@ -88,7 +89,7 @@ def tile_behavioural_box_predictor_s4_kernel(
             nc.sync.dma_start(out=off[:], in_=offset.partition_broadcast(P))
 
             def permute(c):
-                scales = vs_ab[c // 2][:, :, 512 * (c % 2) : 512 * (c % 2 + 1)]
+                scales = vs0[:] if c == 0 else vs123[:, :, 512 * (c - 1) : 512 * c]
                 if c == 0:
                     for t in range(4):
                         nc.vector.tensor_copy(
@@ -120,7 +121,7 @@ def tile_behavioural_box_predictor_s4_kernel(
                             lhsT=vp[c][:, t, g, :].bitcast(FP4X4),
                             lhsT_scale=vsp[c][:, t, g, :],
                             rhs=xw[h][:, g, :].bitcast(FP4X4),
-                            rhs_scale=xs[:, g, 512 * h : 512 * h + 512],
+                            rhs_scale=xs[h][:, g, :],
                             start=(g == 0),
                             stop=(g == 1),
                         )
@@ -143,8 +144,8 @@ def tile_behavioural_box_predictor_s4_kernel(
                 if k == 0:
                     gr[h, c] = work.tile([P, 512, 4], BF16, name="gr", tag="gr", bufs=4, align_bytes=256)
                 cols = slice(256 * k, 256 * k + 256)
-                dst = gr[h, c][:, cols, :]
-                src = cl[h, c][:, :, cols].rearrange("p t m -> p m t")
+                dst = gr[h, c][:, cols, :].rearrange("p (a i) t -> p a t i", i=4)
+                src = cl[h, c][:, :, cols].rearrange("p t (a i) -> p a t i", i=4)
                 if eng == "v":
                     nc.vector.tensor_copy(out=dst, in_=src)
                 else:
@@ -159,53 +160,50 @@ def tile_behavioural_box_predictor_s4_kernel(
                 )
 
             acc = {}
+            ot = {}
 
-            def mm2(i, f, g, first, last):
-                h, cols = i // 4, slice(128 * (i % 4), 128 * (i % 4) + 128)
+            def mm2(i, cols, g, first, last):
+                h, rows = i // 4, slice(128 * (i % 4), 128 * (i % 4) + 128)
+                lo_f, hi_f = cols
                 if first:
-                    acc[i, f] = psum.tile([P, 512], F32, name="ps", tag="ps")
+                    acc[i, cols] = psum.tile([P, hi_f - lo_f], F32, name="ps", tag="ps")
                 nc.tensor.matmul_mx(
-                    out=acc[i, f][:],
-                    lhsT=bc[h][g][:, cols].bitcast(FP8X4),
-                    lhsT_scale=bs[h][g][:, cols],
-                    rhs=hw[g][:, 2048 * f : 2048 * f + 2048].bitcast(FP8X4),
-                    rhs_scale=hs[4 * g : P, 512 * f : 512 * f + 512],
+                    out=acc[i, cols][:],
+                    lhsT=bc[h][g][:, rows].bitcast(FP8X4),
+                    lhsT_scale=bs[h][g][:, rows],
+                    rhs=hw[g][:, 4 * lo_f : 4 * hi_f].bitcast(FP8X4),
+                    rhs_scale=hs[4 * g : P, lo_f:hi_f],
                     start=first,
                     stop=last,
                 )
 
-            ot = {}
-
-            def finish(i, f):
-                if f == 0:
+            def finish(i, cols):
+                lo_f, hi_f = cols
+                if lo_f == 0:
                     ot[i] = work.tile([P, 1024], F32, name="ot", tag="ot", bufs=4, align_bytes=256)
-                cols = slice(512 * f, 512 * f + 512)
-                nc.vector.tensor_tensor(out=ot[i][:, cols], in0=acc[i, f][:], in1=off[:, cols], op=ALU.add)
+                f = slice(lo_f, hi_f)
+                nc.vector.tensor_tensor(out=ot[i][:, f], in0=acc[i, cols][:], in1=off[:, f], op=ALU.add)
                 if i == 7:
-                    nc.sync.dma_start(out=out[P * i : P * i + P, cols], in_=ot[i][:, cols])
-                elif f == 1:
+                    nc.sync.dma_start(out=out[P * i : P * i + P, f], in_=ot[i][:, f])
+                elif hi_f == 1024:
                     nc.sync.dma_start(out=out[P * i : P * i + P, :], in_=ot[i][:])
 
-            def stage2_block(i0, order, group_major):
-                tiles = [(i, f) for i in (i0, i0 + 1) for f in range(2)]
-                if group_major:
-                    for n, g in enumerate(order):
-                        for i, f in tiles:
-                            mm2(i, f, g, n == 0, n == 3)
-                else:
-                    for i, f in tiles:
-                        for n, g in enumerate(order):
-                            mm2(i, f, g, n == 0, n == 3)
+            HALVES = ((0, 512), (512, 1024))
+            LAST = ((0, 512), (512, 768), (768, 1024))
 
-            def pipe(new, old, eng):
-                clamp(*new, 0)
-                clamp(*new, 1)
-                weave(*old, 0, "v")
-                clamp(*new, 2)
-                weave(*old, 1, "v")
-                clamp(*new, 3)
-                quantize(*old, 0)
-                quantize(*old, 1)
+            def group_major(i0, order=(0, 1, 2, 3)):
+                for n, g in enumerate(order):
+                    for i in (i0, i0 + 1):
+                        for cols in HALVES:
+                            mm2(i, cols, g, n == 0, n == 3)
+
+            def clamps(h, c):
+                for t in range(4):
+                    clamp(h, c, t)
+
+            def finishes(i):
+                for cols in LAST if i == 7 else HALVES:
+                    finish(i, cols)
 
             permute(0)
             stage1(0, 0)
@@ -214,56 +212,65 @@ def tile_behavioural_box_predictor_s4_kernel(
             permute(2)
             nc.vector.tensor_scalar(out=hi[:], in0=box_bf[:].rearrange("p c t -> p (c t)"), scalar1=1.0, scalar2=None, op0=ALU.mult)
             nc.vector.tensor_scalar(out=lo[:], in0=box_bf[:].rearrange("p c t -> p (c t)"), scalar1=-1.0, scalar2=None, op0=ALU.mult)
-            permute(3)
-            for t in range(4):
-                clamp(0, 0, t)
             stage1(0, 2)
+            permute(3)
+            clamps(0, 0)
+            clamps(0, 1)
             stage1(0, 3)
-            pipe((0, 1), (0, 0), "v")
+            weave(0, 0, 0, "v")
+            weave(0, 1, 0, "v")
+            quantize(0, 0, 0)
+            clamps(0, 2)
+            quantize(0, 1, 0)
+            weave(0, 0, 1, "s")
             stage1(1, 0)
-            pipe((0, 2), (0, 1), "v")
+            weave(0, 1, 1, "s")
             stage1(1, 1)
-            pipe((0, 3), (0, 2), "v")
             stage1(1, 2)
-            pipe((1, 0), (0, 3), "v")
             stage1(1, 3)
-            stage2_block(0, (0, 1, 2, 3), True)
-            weave(1, 0, 0, "s")
-            weave(1, 0, 1, "s")
-            for t in range(4):
-                clamp(1, 1, t)
-            weave(1, 1, 0, "s")
-            weave(1, 1, 1, "s")
-            for t in range(4):
-                clamp(1, 2, t)
-            weave(1, 2, 0, "s")
-            weave(1, 2, 1, "s")
+            weave(0, 2, 0, "v")
+            clamps(0, 3)
+            quantize(0, 2, 0)
+            weave(0, 3, 0, "v")
+            quantize(0, 0, 1)
+            clamp(1, 0, 0)
+            clamp(1, 0, 1)
+            quantize(0, 3, 0)
+            clamp(1, 0, 2)
+            clamp(1, 0, 3)
+            weave(0, 2, 1, "v")
+            quantize(0, 1, 1)
+            weave(0, 3, 1, "v")
+            quantize(0, 2, 1)
+            clamps(1, 1)
+            quantize(0, 3, 1)
+            clamps(1, 2)
+            for k in range(2):
+                for c in range(3):
+                    weave(1, c, k, "s")
+                if k == 0:
+                    clamps(1, 3)
+                weave(1, 3, k, "s")
+            group_major(0)
             quantize(1, 0, 0)
-            quantize(1, 0, 1)
-            for t in range(4):
-                clamp(1, 3, t)
-            finish(0, 0)
-            weave(1, 3, 0, "v")
-            finish(0, 1)
-            weave(1, 3, 1, "v")
-            quantize(1, 3, 0)
-            finish(1, 0)
-            quantize(1, 3, 1)
-            finish(1, 1)
+            finishes(0)
             quantize(1, 1, 0)
-            quantize(1, 1, 1)
-            stage2_block(2, (0, 1, 2, 3), False)
-            finish(2, 0)
-            finish(2, 1)
+            finishes(1)
             quantize(1, 2, 0)
+            group_major(2)
+            quantize(1, 3, 0)
+            finishes(2)
+            quantize(1, 0, 1)
+            finishes(3)
+            quantize(1, 1, 1)
+            group_major(4)
             quantize(1, 2, 1)
-            finish(3, 0)
-            finish(3, 1)
-            stage2_block(4, (0, 1, 3, 2), True)
-            for i in (4, 5):
-                for f in range(2):
-                    finish(i, f)
-            stage2_block(6, (0, 1, 2, 3), False)
+            finishes(4)
+            quantize(1, 3, 1)
+            finishes(5)
             for i in (6, 7):
-                for f in range(2):
-                    finish(i, f)
+                for cols in LAST if i == 7 else HALVES:
+                    for g in range(4):
+                        mm2(i, cols, g, g == 0, g == 3)
+            finishes(6)
+            finishes(7)

@@ -33,10 +33,9 @@ def tile_behavioural_box_predictor_s4_kernel(
         vw0 = kept([P, 2, 1024], U8, "vw0")
         vw1 = kept([P, 2, 1024], U8, "vw1")
         vw23 = kept([P, 2, 2048], U8, "vw23")
-        vs0 = kept([P, 2, 512], U8, "vs0")
-        vs123 = kept([P, 2, 1536], U8, "vs123")
+        vs_ab = [kept([P, 2, 1024], U8, "vs%d" % i) for i in range(2)]
         xw = [kept([P, 2, 1024], U8, "xw%d" % i) for i in range(2)]
-        xs = [kept([P, 2, 512], U8, "xs%d" % i) for i in range(2)]
+        xs = kept([P, 2, 1024], U8, "xs")
         vp = [kept([P, 4, 2, 256], U8, "vp%d" % c) for c in range(4)]
         vsp = [kept([P, 4, 2, 128], U8, "vsp%d" % c) for c in range(4)]
         hw = [kept([P, 4096], U8, "hw%d" % g) for g in range(4)]
@@ -67,21 +66,19 @@ def tile_behavioural_box_predictor_s4_kernel(
         with tc.manual_schedule():
             load(nc.gpsimd, vw0[:], pw[:, :, 0:1024])
             load(nc.gpsimd, xw[0][:], xwr[:, :, 0:1024])
-            for plane in (vs0, xs[0], vs123, xs[1]):
+            for plane in (vs_ab[0], xs):
                 nc.vector.memset(plane[:].bitcast(I32), 0)
             for q in range(4):
-                scale_rows(nc.sync, vs0, pinv_scales[:, :, 0:512], q)
-            for q in range(4):
-                scale_rows(nc.scalar, xs[0], past_scales[:, :, 0:512], q)
-            nc.gpsimd.memset(hs[:].bitcast(I32), 0)
+                scale_rows(nc.sync, vs_ab[0], pinv_scales[:, :, 0:1024], q)
+                scale_rows(nc.scalar, xs, past_scales, q)
+            load(nc.gpsimd, xw[1][:], xwr[:, :, 1024:2048])
+            for plane in (vs_ab[1], hs):
+                nc.gpsimd.memset(plane[:].bitcast(I32), 0)
             load(nc.sync, vw1[:], pw[:, :, 1024:2048])
-            load(nc.sync, vw23[:], pw[:, :, 2048:4096])
             for q in range(4):
-                scale_rows(nc.sync, vs123, pinv_scales[:, :, 512:2048], q)
+                scale_rows(nc.sync, vs_ab[1], pinv_scales[:, :, 1024:2048], q)
             nc.sync.dma_start(out=box_bf[:], in_=box.rearrange("(c p t) -> p c t", p=P, t=4))
-            load(nc.sync, xw[1][:], xwr[:, :, 1024:2048])
-            for q in range(4):
-                scale_rows(nc.sync, xs[1], past_scales[:, :, 512:1024], q)
+            load(nc.sync, vw23[:], pw[:, :, 2048:4096])
             for g in range(4):
                 load(nc.sync, hw[g][:], fut_words[g].rearrange("p n t -> p (n t)"))
             for q in range(4):
@@ -89,7 +86,7 @@ def tile_behavioural_box_predictor_s4_kernel(
             nc.sync.dma_start(out=off[:], in_=offset.partition_broadcast(P))
 
             def permute(c):
-                scales = vs0[:] if c == 0 else vs123[:, :, 512 * (c - 1) : 512 * c]
+                scales = vs_ab[c // 2][:, :, 512 * (c % 2) : 512 * (c % 2 + 1)]
                 if c == 0:
                     for t in range(4):
                         nc.vector.tensor_copy(
@@ -112,7 +109,7 @@ def tile_behavioural_box_predictor_s4_kernel(
             gr = {}
 
             def stage1(h, c):
-                s32[h, c] = work.tile([P, 4, 512], F32, name="s32", tag="s32", bufs=6, align_bytes=256)
+                s32[h, c] = work.tile([P, 4, 512], F32, name="s32", tag="s32", bufs=8, align_bytes=256)
                 for t in range(4):
                     ps = psum.tile([P, 512], F32, name="ps", tag="ps")
                     for g in range(2):
@@ -121,15 +118,15 @@ def tile_behavioural_box_predictor_s4_kernel(
                             lhsT=vp[c][:, t, g, :].bitcast(FP4X4),
                             lhsT_scale=vsp[c][:, t, g, :],
                             rhs=xw[h][:, g, :].bitcast(FP4X4),
-                            rhs_scale=xs[h][:, g, :],
+                            rhs_scale=xs[:, g, 512 * h : 512 * h + 512],
                             start=(g == 0),
                             stop=(g == 1),
                         )
                     nc.scalar.copy(out=s32[h, c][:, t, :], in_=ps[:])
 
             def clamp(h, c, t):
-                if t == 0:
-                    cl[h, c] = work.tile([P, 4, 512], BF16, name="cl", tag="cl", bufs=5, align_bytes=256)
+                if (h, c) not in cl:
+                    cl[h, c] = work.tile([P, 4, 512], BF16, name="cl", tag="cl", bufs=8, align_bytes=256)
                 j = 4 * c + t
                 nc.vector.tensor_scalar(
                     out=cl[h, c][:, t, :],
@@ -142,7 +139,7 @@ def tile_behavioural_box_predictor_s4_kernel(
 
             def weave(h, c, k, eng):
                 if k == 0:
-                    gr[h, c] = work.tile([P, 512, 4], BF16, name="gr", tag="gr", bufs=4, align_bytes=256)
+                    gr[h, c] = work.tile([P, 512, 4], BF16, name="gr", tag="gr", bufs=6, align_bytes=256)
                 cols = slice(256 * k, 256 * k + 256)
                 dst = gr[h, c][:, cols, :].rearrange("p (a i) t -> p a t i", i=4)
                 src = cl[h, c][:, :, cols].rearrange("p t (a i) -> p a t i", i=4)
@@ -207,56 +204,59 @@ def tile_behavioural_box_predictor_s4_kernel(
 
             permute(0)
             stage1(0, 0)
+            stage1(1, 0)
             permute(1)
-            stage1(0, 1)
-            permute(2)
             nc.vector.tensor_scalar(out=hi[:], in0=box_bf[:].rearrange("p c t -> p (c t)"), scalar1=1.0, scalar2=None, op0=ALU.mult)
             nc.vector.tensor_scalar(out=lo[:], in0=box_bf[:].rearrange("p c t -> p (c t)"), scalar1=-1.0, scalar2=None, op0=ALU.mult)
-            stage1(0, 2)
-            permute(3)
             clamps(0, 0)
-            clamps(0, 1)
-            stage1(0, 3)
-            weave(0, 0, 0, "v")
-            weave(0, 1, 0, "v")
-            quantize(0, 0, 0)
-            clamps(0, 2)
-            quantize(0, 1, 0)
-            weave(0, 0, 1, "s")
-            stage1(1, 0)
-            weave(0, 1, 1, "s")
+            stage1(0, 1)
             stage1(1, 1)
+            clamps(1, 0)
+            permute(2)
+            weave(0, 0, 0, "v")
+            weave(0, 0, 1, "v")
+            quantize(0, 0, 0)
+            stage1(0, 2)
             stage1(1, 2)
-            stage1(1, 3)
-            weave(0, 2, 0, "v")
-            clamps(0, 3)
-            quantize(0, 2, 0)
-            weave(0, 3, 0, "v")
+            clamps(0, 1)
             quantize(0, 0, 1)
-            clamp(1, 0, 0)
-            clamp(1, 0, 1)
-            quantize(0, 3, 0)
-            clamp(1, 0, 2)
-            clamp(1, 0, 3)
-            weave(0, 2, 1, "v")
-            quantize(0, 1, 1)
-            weave(0, 3, 1, "v")
-            quantize(0, 2, 1)
-            clamps(1, 1)
-            quantize(0, 3, 1)
-            clamps(1, 2)
-            for k in range(2):
-                for c in range(3):
-                    weave(1, c, k, "s")
-                if k == 0:
-                    clamps(1, 3)
-                weave(1, 3, k, "s")
-            group_major(0)
+            permute(3)
+            stage1(0, 3)
+            weave(0, 1, 0, "v")
+            weave(1, 0, 0, "v")
+            quantize(0, 1, 0)
+            clamps(0, 2)
             quantize(1, 0, 0)
-            finishes(0)
+            clamps(1, 1)
+            weave(0, 2, 0, "v")
+            clamp(0, 3, 0)
+            clamp(0, 3, 1)
+            weave(0, 1, 1, "s")
+            stage1(1, 3)
+            quantize(0, 2, 0)
+            clamp(0, 3, 2)
+            clamp(0, 3, 3)
+            weave(0, 2, 1, "s")
+            quantize(0, 1, 1)
+            weave(0, 3, 0, "v")
+            clamp(1, 2, 0)
+            clamp(1, 2, 1)
+            quantize(0, 3, 0)
+            quantize(0, 2, 1)
+            weave(0, 3, 1, "v")
+            clamp(1, 2, 2)
+            clamp(1, 2, 3)
+            quantize(0, 3, 1)
+            clamps(1, 3)
+            for c, k in ((1, 0), (2, 0), (3, 0), (0, 1), (1, 1), (2, 1)):
+                weave(1, c, k, "s")
+            group_major(0)
             quantize(1, 1, 0)
+            finishes(0)
+            weave(1, 3, 1, "v")
             finishes(1)
             quantize(1, 2, 0)
+            quantize(1, 3, 1)
             group_major(2)
             quantize(1, 3, 0)
             finishes(2)
@@ -266,7 +266,6 @@ def tile_behavioural_box_predictor_s4_kernel(
             group_major(4)
             quantize(1, 2, 1)
             finishes(4)
-            quantize(1, 3, 1)
             finishes(5)
             for i in (6, 7):
                 for cols in LAST if i == 7 else HALVES:

from contextlib import ExitStack

import concourse.mybir as mybir

M, K, N, F = 1024, 1024, 2048, 1024
FLOPS = 2 * M * K * N + 2 * M * N * F
BYTES = 8034304

F32 = mybir.dt.float32
BF16 = mybir.dt.bfloat16
U32 = mybir.dt.uint32
I32 = mybir.dt.int32
U8 = mybir.dt.uint8
FP8X4 = mybir.dt.float8_e4m3fn_x4
FP4X4 = mybir.dt.float4_e2m1fn_x4
ALU = mybir.AluOpType

P = 128


def tile_behavioural_box_predictor_s4_kernel(
    tc, past_words, past_scales, pinv_words, pinv_scales, box, fut_words, fut_scales, offset, out
):
    nc = tc.nc
    with ExitStack() as ctx:
        keep = ctx.enter_context(tc.tile_pool(name="keep", bufs=1))
        work = ctx.enter_context(tc.tile_pool(name="work", bufs=3))
        psum = ctx.enter_context(tc.psum_pool(name="psum", bufs=8))

        def kept(shape, dtype, name):
            return keep.tile(shape, dtype, name=name, tag=name, align_bytes=256)

        vw0 = kept([P, 2, 1024], U8, "vw0")
        vw1 = kept([P, 2, 1024], U8, "vw1")
        vw23 = kept([P, 2, 2048], U8, "vw23")
        vs_ab = [kept([P, 2, 1024], U8, "vs%d" % i) for i in range(2)]
        xw = [kept([P, 2, 1024], U8, "xw%d" % i) for i in range(2)]
        xs = kept([P, 2, 1024], U8, "xs")
        vp = [kept([P, 4, 2, 256], U8, "vp%d" % c) for c in range(4)]
        vsp = [kept([P, 4, 2, 128], U8, "vsp%d" % c) for c in range(4)]
        hw = [kept([P, 4096], U8, "hw%d" % g) for g in range(4)]
        hs = kept([P, 1024], U8, "hs")
        box_bf = kept([P, 4, 4], BF16, "box_bf")
        hi = kept([P, 16], F32, "hi")
        lo = kept([P, 16], F32, "lo")
        off = kept([P, 1024], BF16, "off")
        bc = [[kept([P, 512], U32, "bc%d_%d" % (h, c)) for c in range(4)] for h in range(2)]
        bs = [[kept([P, 512], U8, "bs%d_%d" % (h, c)) for c in range(4)] for h in range(2)]

        def raw(c):
            if c == 0:
                return vw0[:]
            if c == 1:
                return vw1[:]
            return vw23[:, :, 1024 * (c - 2) : 1024 * (c - 1)]

        pw = pinv_words.rearrange("g p b -> p g b")
        xwr = past_words.rearrange("g p b -> p g b")

        def load(eng, dst, src):
            eng.dma_start(out=dst.bitcast(I32), in_=src.bitcast(I32))

        def scale_rows(eng, dst, src, q):
            load(eng, dst[32 * q : 32 * q + 4], src[:, 4 * q : 4 * q + 4, :].rearrange("g r n -> r g n"))

        with tc.manual_schedule():
            load(nc.gpsimd, vw0[:], pw[:, :, 0:1024])
            load(nc.gpsimd, xw[0][:], xwr[:, :, 0:1024])
            for plane in (vs_ab[0], xs):
                nc.vector.memset(plane[:].bitcast(I32), 0)
            for q in range(4):
                scale_rows(nc.sync, vs_ab[0], pinv_scales[:, :, 0:1024], q)
                scale_rows(nc.scalar, xs, past_scales, q)
            load(nc.gpsimd, xw[1][:], xwr[:, :, 1024:2048])
            for plane in (vs_ab[1], hs):
                nc.gpsimd.memset(plane[:].bitcast(I32), 0)
            load(nc.sync, vw1[:], pw[:, :, 1024:2048])
            for q in range(4):
                scale_rows(nc.sync, vs_ab[1], pinv_scales[:, :, 1024:2048], q)
            nc.sync.dma_start(out=box_bf[:], in_=box.rearrange("(c p t) -> p c t", p=P, t=4))
            load(nc.sync, vw23[:], pw[:, :, 2048:4096])
            for g in range(4):
                load(nc.sync, hw[g][:], fut_words[g].rearrange("p n t -> p (n t)"))
            for q in range(4):
                load(nc.sync, hs[32 * q : 32 * q + 16, :], fut_scales[:, 4 * q : 4 * q + 4, :])
            nc.sync.dma_start(out=off[:], in_=offset.partition_broadcast(P))

            def permute(c):
                scales = vs_ab[c // 2][:, :, 512 * (c % 2) : 512 * (c % 2 + 1)]
                if c == 0:
                    for t in range(4):
                        nc.vector.tensor_copy(
                            out=vp[c][:, t].rearrange("p g (m b) -> p g m b", b=2),
                            in_=raw(c).rearrange("p g (m t b) -> p t g m b", t=4, b=2)[:, t],
                        )
                        nc.vector.tensor_copy(
                            out=vsp[c][:, t], in_=scales.rearrange("p g (m t) -> p t g m", t=4)[:, t]
                        )
                else:
                    for g in range(2):
                        nc.vector.tensor_copy(
                            out=vp[c][:, :, g].rearrange("p t (m b) -> p t m b", b=2),
                            in_=raw(c)[:, g].rearrange("p (m t b) -> p t m b", t=4, b=2),
                        )
                    nc.vector.tensor_copy(out=vsp[c][:], in_=scales.rearrange("p g (m t) -> p t g m", t=4))

            s32 = {}
            cl = {}
            gr = {}

            def stage1(h, c):
                s32[h, c] = work.tile([P, 4, 512], F32, name="s32", tag="s32", bufs=8, align_bytes=256)
                for t in range(4):
                    ps = psum.tile([P, 512], F32, name="ps", tag="ps")
                    for g in range(2):
                        nc.tensor.matmul_mx(
                            out=ps[:],
                            lhsT=vp[c][:, t, g, :].bitcast(FP4X4),
                            lhsT_scale=vsp[c][:, t, g, :],
                            rhs=xw[h][:, g, :].bitcast(FP4X4),
                            rhs_scale=xs[:, g, 512 * h : 512 * h + 512],
                            start=(g == 0),
                            stop=(g == 1),
                        )
                    nc.scalar.copy(out=s32[h, c][:, t, :], in_=ps[:])

            def clamp(h, c, t):
                if (h, c) not in cl:
                    cl[h, c] = work.tile([P, 4, 512], BF16, name="cl", tag="cl", bufs=8, align_bytes=256)
                j = 4 * c + t
                nc.vector.tensor_scalar(
                    out=cl[h, c][:, t, :],
                    in0=s32[h, c][:, t, :],
                    scalar1=hi[:, j : j + 1],
                    scalar2=lo[:, j : j + 1],
                    op0=ALU.min,
                    op1=ALU.max,
                )

            def weave(h, c, k, eng):
                if k == 0:
                    gr[h, c] = work.tile([P, 512, 4], BF16, name="gr", tag="gr", bufs=6, align_bytes=256)
                cols = slice(256 * k, 256 * k + 256)
                dst = gr[h, c][:, cols, :].rearrange("p (a i) t -> p a t i", i=4)
                src = cl[h, c][:, :, cols].rearrange("p t (a i) -> p a t i", i=4)
                if eng == "v":
                    nc.vector.tensor_copy(out=dst, in_=src)
                else:
                    nc.scalar.copy(out=dst, in_=src)

            def quantize(h, c, k):
                cols = slice(256 * k, 256 * k + 256)
                nc.vector.quantize_mx(
                    out=bc[h][c][:, cols].bitcast(FP8X4),
                    scales=bs[h][c][:, cols],
                    in_=gr[h, c][:, cols, :].rearrange("p m t -> p (m t)"),
                )

            acc = {}
            ot = {}

            def mm2(i, cols, g, first, last):
                h, rows = i // 4, slice(128 * (i % 4), 128 * (i % 4) + 128)
                lo_f, hi_f = cols
                if first:
                    acc[i, cols] = psum.tile([P, hi_f - lo_f], F32, name="ps", tag="ps")
                nc.tensor.matmul_mx(
                    out=acc[i, cols][:],
                    lhsT=bc[h][g][:, rows].bitcast(FP8X4),
                    lhsT_scale=bs[h][g][:, rows],
                    rhs=hw[g][:, 4 * lo_f : 4 * hi_f].bitcast(FP8X4),
                    rhs_scale=hs[4 * g : P, lo_f:hi_f],
                    start=first,
                    stop=last,
                )

            def finish(i, cols):
                lo_f, hi_f = cols
                if lo_f == 0:
                    ot[i] = work.tile([P, 1024], F32, name="ot", tag="ot", bufs=4, align_bytes=256)
                f = slice(lo_f, hi_f)
                nc.vector.tensor_tensor(out=ot[i][:, f], in0=acc[i, cols][:], in1=off[:, f], op=ALU.add)
                if i == 7:
                    nc.sync.dma_start(out=out[P * i : P * i + P, f], in_=ot[i][:, f])
                elif hi_f == 1024:
                    nc.sync.dma_start(out=out[P * i : P * i + P, :], in_=ot[i][:])

            HALVES = ((0, 512), (512, 1024))
            LAST = ((0, 512), (512, 768), (768, 1024))

            def group_major(i0, order=(0, 1, 2, 3)):
                for n, g in enumerate(order):
                    for i in (i0, i0 + 1):
                        for cols in HALVES:
                            mm2(i, cols, g, n == 0, n == 3)

            def clamps(h, c):
                for t in range(4):
                    clamp(h, c, t)

            def finishes(i):
                for cols in LAST if i == 7 else HALVES:
                    finish(i, cols)

            permute(0)
            stage1(0, 0)
            stage1(1, 0)
            permute(1)
            nc.vector.tensor_scalar(out=hi[:], in0=box_bf[:].rearrange("p c t -> p (c t)"), scalar1=1.0, scalar2=None, op0=ALU.mult)
            nc.vector.tensor_scalar(out=lo[:], in0=box_bf[:].rearrange("p c t -> p (c t)"), scalar1=-1.0, scalar2=None, op0=ALU.mult)
            clamps(0, 0)
            stage1(0, 1)
            stage1(1, 1)
            clamps(1, 0)
            permute(2)
            weave(0, 0, 0, "v")
            weave(0, 0, 1, "v")
            quantize(0, 0, 0)
            stage1(0, 2)
            stage1(1, 2)
            clamps(0, 1)
            quantize(0, 0, 1)
            permute(3)
            stage1(0, 3)
            weave(0, 1, 0, "v")
            weave(1, 0, 0, "v")
            quantize(0, 1, 0)
            clamps(0, 2)
            quantize(1, 0, 0)
            clamps(1, 1)
            weave(0, 2, 0, "v")
            clamp(0, 3, 0)
            clamp(0, 3, 1)
            weave(0, 1, 1, "s")
            stage1(1, 3)
            quantize(0, 2, 0)
            clamp(0, 3, 2)
            clamp(0, 3, 3)
            weave(0, 2, 1, "s")
            quantize(0, 1, 1)
            weave(0, 3, 0, "v")
            clamp(1, 2, 0)
            clamp(1, 2, 1)
            quantize(0, 3, 0)
            quantize(0, 2, 1)
            weave(0, 3, 1, "v")
            clamp(1, 2, 2)
            clamp(1, 2, 3)
            quantize(0, 3, 1)
            clamps(1, 3)
            for c, k in ((1, 0), (2, 0), (3, 0), (0, 1), (1, 1), (2, 1)):
                weave(1, c, k, "s")
            group_major(0)
            quantize(1, 1, 0)
            finishes(0)
            weave(1, 3, 1, "v")
            finishes(1)
            quantize(1, 2, 0)
            quantize(1, 3, 1)
            group_major(2)
            quantize(1, 3, 0)
            finishes(2)
            quantize(1, 0, 1)
            finishes(3)
            quantize(1, 1, 1)
            group_major(4)
            quantize(1, 2, 1)
            finishes(4)
            finishes(5)
            for i in (6, 7):
                for cols in LAST if i == 7 else HALVES:
                    for g in range(4):
                        mm2(i, cols, g, g == 0, g == 3)
            finishes(6)
            finishes(7)
